import numpy as np
import ml_dtypes


def mxq(x, axis, fmt="e4m3"):
    dtype, down = {"e4m3": (ml_dtypes.float8_e4m3fn, 7), "e5m2": (ml_dtypes.float8_e5m2, 14)}[fmt]
    v = np.moveaxis(np.asarray(x, np.float32).astype(ml_dtypes.bfloat16).astype(np.float64), axis, -1)
    blocks = v.reshape(v.shape[:-1] + (-1, 32))
    amax = np.abs(blocks).max(-1, keepdims=True)
    byte = np.maximum(np.where(amax > 0, np.frexp(amax)[1] - 1 + 127, 0) - down, 1)
    scale = np.exp2(byte - 127.0)
    codes = (blocks / scale).astype(np.float32).astype(dtype).astype(np.float64)
    return np.moveaxis((codes * scale).reshape(v.shape), -1, axis)


WIDE = False


def mx_kscale(k):
    if not WIDE:
        return np.ones(k)
    levels = np.array([10, -10, 5, -5, 0])
    if k % 512:
        return np.exp2(np.random.permutation(np.resize(levels, k // 32))).repeat(32)
    a = np.empty((k // 512, 16))
    for p in range(k // 512):
        a[p, :8] = np.random.permutation(np.resize(levels, 8))
        for g in range(8):
            far = levels[np.abs(levels - a[p, g]) >= 10]
            a[p, g + 8] = far[np.random.randint(len(far))]
    return np.exp2(a.ravel()).repeat(32)


def f64(x):
    return np.asarray(x).astype(np.float64)


def striped(idx):
    return np.tile(idx.reshape(-1, 16).T, (8, 1)).astype(np.uint16)


def unstriped(offs):
    return offs[:16].T.reshape(-1).astype(np.int64)


def pack_weight(w):
    k, n = w.shape
    w = f64(np.asarray(w, np.float32).astype(ml_dtypes.bfloat16)).reshape(k // 32, 32, n)
    amax = np.abs(w).max(1)
    byte = np.clip(np.where(amax > 0, np.frexp(amax)[1] - 1 + 127 - 7, 1), 1, 254)
    scaled = (w * np.exp2(127.0 - byte)[:, None, :]).reshape(k, n).astype(np.float32)
    words = np.ascontiguousarray(scaled.reshape(k // 512, 128, 4, n).transpose(0, 1, 3, 2)).astype(ml_dtypes.float8_e4m3fn).view(np.uint8)
    return words, np.ascontiguousarray(byte.astype(np.uint8).reshape(k // 512, 16, n))


def unpack_weight(words, scales):
    g, p, n, _ = words.shape
    vals = np.ascontiguousarray(words).view(ml_dtypes.float8_e4m3fn).astype(np.float64) * np.repeat(np.exp2(scales.astype(np.float64) - 127.0), 8, axis=1)[..., None]
    return vals.transpose(0, 1, 3, 2).reshape(g * 512, n)


def gelu(v):
    return 0.5 * v * (1.0 + np.tanh(np.sqrt(2.0 / np.pi) * (v + 0.044715 * v**3)))


K, T, D, S, V, N = 1536, 2048, 8, 512, 64, 256


def setup_inputs():
    n = np.random.standard_normal
    s = mx_kscale(K)[:, None]
    words, scales = pack_weight(n((K, N)) / np.sqrt(K) / s)
    return {
        "xT": (n((K, T)) * s).astype(np.float32),
        "w_words": words,
        "w_scales": scales,
        "b": (0.3 * n((N, 1))).astype(np.float32),
        "offs": striped(np.random.permutation(T)[:S]),
    }


def reference(xT, w_words, w_scales, b, offs):
    w = unpack_weight(w_words, w_scales)
    idx = unstriped(offs)
    xq = mxq(f64(xT)[:, idx], 0, "e4m3")
    y = w.T @ xq
    y = gelu(y + f64(b))
    return y.reshape(N, V, D).max(axis=2)

@@ -1,0 +1,113 @@
+from contextlib import ExitStack
+
+import concourse.mybir as mybir
+
+K, T, S, N, D = 1536, 2048, 512, 256, 8
+FLOPS = 2 * K * S * N
+
+F32 = mybir.dt.float32
+BF16 = mybir.dt.bfloat16
+U32 = mybir.dt.uint32
+I32 = mybir.dt.int32
+U16 = mybir.dt.uint16
+U8 = mybir.dt.uint8
+FP8X4 = mybir.dt.float8_e4m3fn_x4
+GELU = mybir.ActivationFunctionType.Gelu_apprx_tanh
+
+P = 128
+PACK = 4
+PASSES = K // (P * PACK)
+M_TILES = N // P
+HALF = S // 2
+COLS = HALF // 16
+
+
+def tile_picked_pool_lin_gelu_sub_e_kernel(tc, xT, w_words, w_scales, b, offs, out):
+    nc = tc.nc
+    with ExitStack() as ctx:
+        keep = ctx.enter_context(tc.tile_pool(name="keep", bufs=1))
+        psum = ctx.enter_context(tc.psum_pool(name="psum", bufs=1))
+
+        offsets = keep.tile([P, S // 16], U16, name="offsets")
+        w_codes = keep.tile([P, PASSES, N], I32, name="w_codes", align_bytes=64)
+        w_scale = keep.tile([P, PASSES, N], U8, name="w_scale", align_bytes=64)
+        bias = keep.tile([P, M_TILES], F32, name="bias")
+        warm = keep.tile([P, 1], F32, name="warm")
+        pooled = keep.tile([P, M_TILES, S // D], F32, name="pooled")
+
+        planes = [[keep.tile([P, T], F32, name=f"x_{a}_{j}") for j in range(PACK)] for a in range(PASSES)]
+        grouped = [keep.tile([P, S, PACK], BF16, name=f"grouped_{a}", align_bytes=64) for a in range(PASSES)]
+        codes = [keep.tile([P, S], U32, name=f"codes_{a}", align_bytes=64) for a in range(PASSES)]
+        scales = [keep.tile([P, S], U8, name=f"scales_{a}", align_bytes=64) for a in range(PASSES)]
+        acc = [[psum.tile([P, HALF], F32, name=f"acc_{m}_{s}") for s in range(2)] for m in range(M_TILES)]
+        act = [[keep.tile([P, HALF], F32, name=f"act_{m}_{s}") for s in range(2)] for m in range(M_TILES)]
+
+        nc.sync.dma_start(offsets[:], offs)
+        x_view = xT.rearrange("(a p j) t -> a p j t", p=P, j=PACK)
+        for a in range(PASSES):
+            for j in range(PACK):
+                nc.sync.dma_start(out=planes[a][j][:], in_=x_view[a, :, j, :])
+        nc.vector.memset(w_scale[:].bitcast(I32), 0)
+        nc.vector.memset(warm[:], 0.0)
+        nc.scalar.activation(warm[:], warm[:], GELU)
+        for q in range(4):
+            nc.sync.dma_start(
+                out=w_scale[32 * q : 32 * q + 4, :, :].bitcast(I32),
+                in_=w_scales[:, 4 * q : 4 * q + 4, :].rearrange("a r m -> r a m").bitcast(I32),
+            )
+        w_view = w_words.rearrange("a p m r -> p a (m r)").bitcast(I32)
+        nc.sync.dma_start(out=w_codes[:, 0:2, :], in_=w_view[:, 0:2, :])
+        nc.sync.dma_start(out=w_codes[:, 2:3, :], in_=w_view[:, 2:3, :])
+        with nc.allow_non_contiguous_dma(reason="one bias value a partition"):
+            nc.sync.dma_start(out=bias[:], in_=b.rearrange("(m p) o -> p (m o)", p=P))
+
+        def multiply(a, s):
+            cols = slice(s * HALF, (s + 1) * HALF)
+            for m in range(M_TILES):
+                rows = slice(m * P, (m + 1) * P)
+                nc.tensor.matmul_mx(
+                    out=acc[m][s][:],
+                    lhsT=w_codes[:, a, rows].bitcast(FP8X4),
+                    lhsT_scale=w_scale[:, a, rows],
+                    rhs=codes[a][:, cols].bitcast(FP8X4),
+                    rhs_scale=scales[a][:, cols],
+                    start=(a == 0),
+                    stop=(a == PASSES - 1),
+                )
+
+        def quantize(a, first, last):
+            nc.vector.quantize_mx(
+                out=codes[a][:, first:last].bitcast(FP8X4),
+                scales=scales[a][:, first:last],
+                in_=grouped[a][:, first:last, :].rearrange("p n j -> p (n j)"),
+            )
+
+        for a in range(PASSES - 1):
+            for j in range(PACK):
+                nc.vector.tensor_copy(grouped[a][:, :, j], planes[a][j][:].indirect(offsets[:]))
+            quantize(a, 0, S)
+            for s in range(2):
+                multiply(a, s)
+
+        a = PASSES - 1
+        for j in range(PACK - 1):
+            nc.vector.tensor_copy(grouped[a][:, :, j], planes[a][j][:].indirect(offsets[:]))
+        for s in range(2):
+            nc.vector.tensor_copy(
+                grouped[a][:, s * HALF : (s + 1) * HALF, PACK - 1],
+                planes[a][PACK - 1][:].indirect(offsets[:, s * COLS : (s + 1) * COLS]),
+            )
+        for s in range(2):
+            quantize(a, s * HALF, (s + 1) * HALF)
+            multiply(a, s)
+        out_view = out.rearrange("(m p) v -> p m v", p=P)
+        for s in range(2):
+            for m in range(M_TILES):
+                nc.scalar.activation(act[m][s][:], acc[m][s][:], GELU, bias=bias[:, m : m + 1])
+                nc.vector.tensor_reduce(
+                    out=pooled[:, m, s * HALF // D : (s + 1) * HALF // D],
+                    in_=act[m][s][:].rearrange("p (v d) -> p v d", d=D),
+                    op=mybir.AluOpType.max,
+                    axis=mybir.AxisListType.X,
+                )
+        nc.sync.dma_start(out=out_view, in_=pooled[:])

@@ -20,6 +20,7 @@ PASSES = K // (P * PACK)
 M_TILES = N // P
 HALF = S // 2
 COLS = HALF // 16
+LOADS = (((0, 2), (2, 4)), ((0, 2), (2, 4)), ((0, 2), (2, 3), (3, 4)))
 
 
 def tile_picked_pool_lin_gelu_sub_e_kernel(tc, xT, w_words, w_scales, b, offs, out):
@@ -35,29 +36,50 @@ def tile_picked_pool_lin_gelu_sub_e_kernel(tc, xT, w_words, w_scales, b, offs, o
         warm = keep.tile([P, 1], F32, name="warm")
         pooled = keep.tile([P, M_TILES, S // D], F32, name="pooled")
 
-        planes = [[keep.tile([P, T], F32, name=f"x_{a}_{j}") for j in range(PACK)] for a in range(PASSES)]
+        blocks = [
+            [keep.tile([P, last - first, T], F32, name=f"x_{a}_{first}") for first, last in LOADS[a]]
+            for a in range(PASSES)
+        ]
         grouped = [keep.tile([P, S, PACK], BF16, name=f"grouped_{a}", align_bytes=64) for a in range(PASSES)]
         codes = [keep.tile([P, S], U32, name=f"codes_{a}", align_bytes=64) for a in range(PASSES)]
         scales = [keep.tile([P, S], U8, name=f"scales_{a}", align_bytes=64) for a in range(PASSES)]
         acc = [[psum.tile([P, HALF], F32, name=f"acc_{m}_{s}") for s in range(2)] for m in range(M_TILES)]
         act = [[keep.tile([P, HALF], F32, name=f"act_{m}_{s}") for s in range(2)] for m in range(M_TILES)]
 
-        nc.sync.dma_start(offsets[:], offs)
-        x_view = xT.rearrange("(a p j) t -> a p j t", p=P, j=PACK)
-        for a in range(PASSES):
-            for j in range(PACK):
-                nc.sync.dma_start(out=planes[a][j][:], in_=x_view[a, :, j, :])
         nc.vector.memset(w_scale[:].bitcast(I32), 0)
         nc.vector.memset(warm[:], 0.0)
         nc.scalar.activation(warm[:], warm[:], GELU)
+
+        x_view = xT.rearrange("(a p j) t -> a p j t", p=P, j=PACK)
+        w_view = w_words.rearrange("a p m r -> p a (m r)").bitcast(I32)
+
+        def load_block(a, i):
+            first, last = LOADS[a][i]
+            nc.sync.dma_start(out=blocks[a][i][:], in_=x_view[a, :, first:last, :])
+
+        def plane(a, j):
+            for (first, last), block in zip(LOADS[a], blocks[a]):
+                if first <= j < last:
+                    return block[:, j - first, :]
+
+        def load_weights(first, last):
+            nc.sync.dma_start(out=w_codes[:, first:last, :], in_=w_view[:, first:last, :])
+
+        nc.sync.dma_start(offsets[:], offs)
+        for a in range(PASSES - 1):
+            for i in range(len(LOADS[a])):
+                load_block(a, i)
+        for i in range(len(LOADS[PASSES - 1]) - 1):
+            load_block(PASSES - 1, i)
         for q in range(4):
             nc.sync.dma_start(
                 out=w_scale[32 * q : 32 * q + 4, :, :].bitcast(I32),
                 in_=w_scales[:, 4 * q : 4 * q + 4, :].rearrange("a r m -> r a m").bitcast(I32),
             )
-        w_view = w_words.rearrange("a p m r -> p a (m r)").bitcast(I32)
-        nc.sync.dma_start(out=w_codes[:, 0:2, :], in_=w_view[:, 0:2, :])
-        nc.sync.dma_start(out=w_codes[:, 2:3, :], in_=w_view[:, 2:3, :])
+        load_weights(0, 1)
+        load_block(PASSES - 1, len(LOADS[PASSES - 1]) - 1)
+        load_weights(1, 2)
+        load_weights(2, 3)
         with nc.allow_non_contiguous_dma(reason="one bias value a partition"):
             nc.sync.dma_start(out=bias[:], in_=b.rearrange("(m p) o -> p (m o)", p=P))
 
@@ -84,18 +106,18 @@ def tile_picked_pool_lin_gelu_sub_e_kernel(tc, xT, w_words, w_scales, b, offs, o
 
         for a in range(PASSES - 1):
             for j in range(PACK):
-                nc.vector.tensor_copy(grouped[a][:, :, j], planes[a][j][:].indirect(offsets[:]))
+                nc.vector.tensor_copy(grouped[a][:, :, j], plane(a, j).indirect(offsets[:]))
             quantize(a, 0, S)
             for s in range(2):
                 multiply(a, s)
 
         a = PASSES - 1
         for j in range(PACK - 1):
-            nc.vector.tensor_copy(grouped[a][:, :, j], planes[a][j][:].indirect(offsets[:]))
+            nc.vector.tensor_copy(grouped[a][:, :, j], plane(a, j).indirect(offsets[:]))
         for s in range(2):
             nc.vector.tensor_copy(
                 grouped[a][:, s * HALF : (s + 1) * HALF, PACK - 1],
-                planes[a][PACK - 1][:].indirect(offsets[:, s * COLS : (s + 1) * COLS]),
+                plane(a, PACK - 1).indirect(offsets[:, s * COLS : (s + 1) * COLS]),
             )
         for s in range(2):
             quantize(a, s * HALF, (s + 1) * HALF)

from contextlib import ExitStack

import concourse.mybir as mybir

K, T, S, N, D = 1536, 2048, 512, 256, 8
FLOPS = 2 * K * S * N

F32 = mybir.dt.float32
BF16 = mybir.dt.bfloat16
U32 = mybir.dt.uint32
I32 = mybir.dt.int32
U16 = mybir.dt.uint16
U8 = mybir.dt.uint8
FP8X4 = mybir.dt.float8_e4m3fn_x4
GELU = mybir.ActivationFunctionType.Gelu_apprx_tanh

P = 128
PACK = 4
PASSES = K // (P * PACK)
M_TILES = N // P
HALF = S // 2
COLS = HALF // 16
LOADS = (((0, 2), (2, 4)), ((0, 2), (2, 4)), ((0, 2), (2, 3), (3, 4)))


def tile_picked_pool_lin_gelu_sub_e_kernel(tc, xT, w_words, w_scales, b, offs, out):
    nc = tc.nc
    with ExitStack() as ctx:
        keep = ctx.enter_context(tc.tile_pool(name="keep", bufs=1))
        psum = ctx.enter_context(tc.psum_pool(name="psum", bufs=1))

        offsets = keep.tile([P, S // 16], U16, name="offsets")
        w_codes = keep.tile([P, PASSES, N], I32, name="w_codes", align_bytes=64)
        w_scale = keep.tile([P, PASSES, N], U8, name="w_scale", align_bytes=64)
        bias = keep.tile([P, M_TILES], F32, name="bias")
        warm = keep.tile([P, 1], F32, name="warm")
        pooled = keep.tile([P, M_TILES, S // D], F32, name="pooled")

        blocks = [
            [keep.tile([P, last - first, T], F32, name=f"x_{a}_{first}") for first, last in LOADS[a]]
            for a in range(PASSES)
        ]
        grouped = [keep.tile([P, S, PACK], BF16, name=f"grouped_{a}", align_bytes=64) for a in range(PASSES)]
        codes = [keep.tile([P, S], U32, name=f"codes_{a}", align_bytes=64) for a in range(PASSES)]
        scales = [keep.tile([P, S], U8, name=f"scales_{a}", align_bytes=64) for a in range(PASSES)]
        acc = [[psum.tile([P, HALF], F32, name=f"acc_{m}_{s}") for s in range(2)] for m in range(M_TILES)]
        act = [[keep.tile([P, HALF], F32, name=f"act_{m}_{s}") for s in range(2)] for m in range(M_TILES)]

        nc.vector.memset(w_scale[:].bitcast(I32), 0)
        nc.vector.memset(warm[:], 0.0)
        nc.scalar.activation(warm[:], warm[:], GELU)

        x_view = xT.rearrange("(a p j) t -> a p j t", p=P, j=PACK)
        w_view = w_words.rearrange("a p m r -> p a (m r)").bitcast(I32)

        def load_block(a, i):
            first, last = LOADS[a][i]
            nc.sync.dma_start(out=blocks[a][i][:], in_=x_view[a, :, first:last, :])

        def plane(a, j):
            for (first, last), block in zip(LOADS[a], blocks[a]):
                if first <= j < last:
                    return block[:, j - first, :]

        def load_weights(first, last):
            nc.sync.dma_start(out=w_codes[:, first:last, :], in_=w_view[:, first:last, :])

        nc.sync.dma_start(offsets[:], offs)
        for a in range(PASSES - 1):
            for i in range(len(LOADS[a])):
                load_block(a, i)
        for i in range(len(LOADS[PASSES - 1]) - 1):
            load_block(PASSES - 1, i)
        for q in range(4):
            nc.sync.dma_start(
                out=w_scale[32 * q : 32 * q + 4, :, :].bitcast(I32),
                in_=w_scales[:, 4 * q : 4 * q + 4, :].rearrange("a r m -> r a m").bitcast(I32),
            )
        load_weights(0, 1)
        load_block(PASSES - 1, len(LOADS[PASSES - 1]) - 1)
        load_weights(1, 2)
        load_weights(2, 3)
        with nc.allow_non_contiguous_dma(reason="one bias value a partition"):
            nc.sync.dma_start(out=bias[:], in_=b.rearrange("(m p) o -> p (m o)", p=P))

        def multiply(a, s):
            cols = slice(s * HALF, (s + 1) * HALF)
            for m in range(M_TILES):
                rows = slice(m * P, (m + 1) * P)
                nc.tensor.matmul_mx(
                    out=acc[m][s][:],
                    lhsT=w_codes[:, a, rows].bitcast(FP8X4),
                    lhsT_scale=w_scale[:, a, rows],
                    rhs=codes[a][:, cols].bitcast(FP8X4),
                    rhs_scale=scales[a][:, cols],
                    start=(a == 0),
                    stop=(a == PASSES - 1),
                )

        def quantize(a, first, last):
            nc.vector.quantize_mx(
                out=codes[a][:, first:last].bitcast(FP8X4),
                scales=scales[a][:, first:last],
                in_=grouped[a][:, first:last, :].rearrange("p n j -> p (n j)"),
            )

        for a in range(PASSES - 1):
            for j in range(PACK):
                nc.vector.tensor_copy(grouped[a][:, :, j], plane(a, j).indirect(offsets[:]))
            quantize(a, 0, S)
            for s in range(2):
                multiply(a, s)

        a = PASSES - 1
        for j in range(PACK - 1):
            nc.vector.tensor_copy(grouped[a][:, :, j], plane(a, j).indirect(offsets[:]))
        for s in range(2):
            nc.vector.tensor_copy(
                grouped[a][:, s * HALF : (s + 1) * HALF, PACK - 1],
                plane(a, PACK - 1).indirect(offsets[:, s * COLS : (s + 1) * COLS]),
            )
        for s in range(2):
            quantize(a, s * HALF, (s + 1) * HALF)
            multiply(a, s)
        out_view = out.rearrange("(m p) v -> p m v", p=P)
        for s in range(2):
            for m in range(M_TILES):
                nc.scalar.activation(act[m][s][:], acc[m][s][:], GELU, bias=bias[:, m : m + 1])
                nc.vector.tensor_reduce(
                    out=pooled[:, m, s * HALF // D : (s + 1) * HALF // D],
                    in_=act[m][s][:].rearrange("p (v d) -> p v d", d=D),
                    op=mybir.AluOpType.max,
                    axis=mybir.AxisListType.X,
                )
        nc.sync.dma_start(out=out_view, in_=pooled[:])
